import numpy as np
import ml_dtypes


def mxq(x, axis, fmt="e4m3"):
    dtype, down = {"e4m3": (ml_dtypes.float8_e4m3fn, 7), "e5m2": (ml_dtypes.float8_e5m2, 14)}[fmt]
    v = np.moveaxis(np.asarray(x, np.float32).astype(ml_dtypes.bfloat16).astype(np.float64), axis, -1)
    blocks = v.reshape(v.shape[:-1] + (-1, 32))
    amax = np.abs(blocks).max(-1, keepdims=True)
    byte = np.maximum(np.where(amax > 0, np.frexp(amax)[1] - 1 + 127, 0) - down, 1)
    scale = np.exp2(byte - 127.0)
    codes = (blocks / scale).astype(np.float32).astype(dtype).astype(np.float64)
    return np.moveaxis((codes * scale).reshape(v.shape), -1, axis)


WIDE = False


def mx_kscale(k):
    if not WIDE:
        return np.ones(k)
    levels = np.array([10, -10, 5, -5, 0])
    if k % 512:
        return np.exp2(np.random.permutation(np.resize(levels, k // 32))).repeat(32)
    a = np.empty((k // 512, 16))
    for p in range(k // 512):
        a[p, :8] = np.random.permutation(np.resize(levels, 8))
        for g in range(8):
            far = levels[np.abs(levels - a[p, g]) >= 10]
            a[p, g + 8] = far[np.random.randint(len(far))]
    return np.exp2(a.ravel()).repeat(32)


def f64(x):
    return np.asarray(x).astype(np.float64)


def striped(idx):
    return np.tile(idx.reshape(-1, 16).T, (8, 1)).astype(np.uint16)


def unstriped(offs):
    return offs[:16].T.reshape(-1).astype(np.int64)


def gelu(v):
    return 0.5 * v * (1.0 + np.tanh(np.sqrt(2.0 / np.pi) * (v + 0.044715 * v**3)))


K, T, S, H, N = 512, 2048, 768, 512, 128


def setup_inputs():
    n = np.random.standard_normal
    s = mx_kscale(K)[:, None]
    u = mx_kscale(H)
    return {
        "xT": (n((K, T)) * s).astype(np.float32),
        "w1": (n((K, H)) / np.sqrt(K) / s * u).astype(np.float32),
        "w2": (n((H, N)) / np.sqrt(H) / u[:, None]).astype(np.float32),
        "offs": striped(np.random.permutation(T)[:S]),
    }


def reference(xT, w1, w2, offs):
    idx = unstriped(offs)
    xq = mxq(f64(xT)[:, idx], 0, "e4m3")
    h = gelu(mxq(f64(w1), 0, "e4m3").T @ xq)
    y = mxq(f64(w2), 0, "e4m3").T @ mxq(h, 0, "e4m3")
    return y

@@ -1,0 +1,181 @@
+from contextlib import ExitStack
+
+import concourse.mybir as mybir
+
+K, T, S, H, N = 512, 2048, 768, 512, 128
+FLOPS = 2 * S * H * (K + N)
+
+F32 = mybir.dt.float32
+BF16 = mybir.dt.bfloat16
+U32 = mybir.dt.uint32
+U16 = mybir.dt.uint16
+U8 = mybir.dt.uint8
+FP8X4 = mybir.dt.float8_e4m3fn_x4
+GELU = mybir.ActivationFunctionType.Gelu_apprx_tanh
+
+P = 128
+PACK = 4
+SLICE = 256
+GROUP = 128
+ALIGN = 64
+
+
+def quantize(nc, codes, scales, values):
+    nc.vector.quantize_mx(out=codes.bitcast(FP8X4), scales=scales, in_=values)
+
+
+def tile_picked_pick_mlp_gelu_sub_e_kernel(tc, xT, w1, w2, offs, out):
+    nc = tc.nc
+    slices = S // SLICE
+    per_slice = SLICE // GROUP
+    groups = S // GROUP
+
+    with ExitStack() as ctx:
+        keep = ctx.enter_context(tc.tile_pool(name="keep", bufs=1))
+        psum = ctx.enter_context(tc.psum_pool(name="psum", bufs=1))
+
+        offsets = keep.tile([P, S // 16], U16, name="offsets")
+        nc.sync.dma_start(offsets[:], offs)
+
+        w1_raw = keep.tile([P, PACK, H], F32, name="w1_raw")
+        nc.sync.dma_start(out=w1_raw[:], in_=w1.rearrange("(p j) h -> p j h", j=PACK))
+        planes = []
+        x_rows = xT.rearrange("(p j) t -> p j t", j=PACK)
+        for j in range(PACK):
+            plane = keep.tile([P, T], F32, name=f"plane{j}")
+            nc.sync.dma_start(out=plane[:], in_=x_rows[:, j, :])
+            planes.append(plane)
+        w2_raw = keep.tile([P, PACK, N], F32, name="w2_raw")
+        nc.sync.dma_start(out=w2_raw[:], in_=w2.rearrange("(p j) n -> p j n", j=PACK))
+
+        probe = keep.tile([P, 1], F32, name="probe")
+        nc.vector.memset(probe[:], 0.0)
+        probe_out = keep.tile([P, 1], F32, name="probe_out")
+        nc.scalar.activation(probe_out[:], probe[:], GELU)
+
+        early = PACK // 2
+        picked = []
+        for s in range(slices):
+            tile = keep.tile([P, PACK, SLICE], F32, name=f"picked{s}")
+            nc.gpsimd.memset(tile[:, early:, :], 0.0)
+            picked.append(tile)
+
+        w1_grouped = keep.tile([P, H * PACK], BF16, name="w1_grouped", align_bytes=ALIGN)
+        w1_to = w1_grouped[:].rearrange("p (t m j) -> p m j t", t=PACK, j=PACK)
+        w1_from = w1_raw[:].rearrange("p j (m t) -> p m j t", t=PACK)
+        for half in range(2):
+            part = slice(half * (P // 2), (half + 1) * (P // 2))
+            nc.scalar.copy(w1_to[:, part], w1_from[:, part])
+        w1_codes = keep.tile([P, H], U32, name="w1_codes", align_bytes=ALIGN)
+        w1_scales = keep.tile([P, H], U8, name="w1_scales", align_bytes=ALIGN)
+        quantize(nc, w1_codes[:], w1_scales[:], w1_grouped[:])
+
+        x_grouped = []
+        for s in range(slices):
+            tile = keep.tile([P, SLICE, PACK], BF16, name=f"x_grouped{s}", align_bytes=ALIGN)
+            x_grouped.append(tile)
+
+        def entries(s):
+            return offsets[:, s * (SLICE // 16) : (s + 1) * (SLICE // 16)]
+
+        for j in range(early):
+            for s in range(slices):
+                nc.vector.tensor_copy(picked[s][:, j, :], planes[j][:].indirect(entries(s)))
+        for s in range(slices):
+            nc.scalar.copy(
+                x_grouped[s][:].rearrange("p (c i) t -> p c t i", i=4),
+                picked[s][:].rearrange("p t (c i) -> p c t i", i=4),
+            )
+        for s in range(slices):
+            nc.vector.tensor_copy(x_grouped[s][:, :, early], planes[early][:].indirect(entries(s)))
+
+        w2_grouped = keep.tile([P, N, PACK], BF16, name="w2_grouped", align_bytes=ALIGN)
+        nc.scalar.copy(
+            w2_grouped[:].rearrange("p (c i) t -> p c t i", i=4), w2_raw[:].rearrange("p t (c i) -> p c t i", i=4)
+        )
+
+        x_codes = keep.tile([P, S], U32, name="x_codes", align_bytes=ALIGN)
+        x_scales = keep.tile([P, S], U8, name="x_scales", align_bytes=ALIGN)
+        h_codes = keep.tile([P, S], U32, name="h_codes", align_bytes=ALIGN)
+        h_scales = keep.tile([P, S], U8, name="h_scales", align_bytes=ALIGN)
+        w2_codes = keep.tile([P, N], U32, name="w2_codes", align_bytes=ALIGN)
+        w2_scales = keep.tile([P, N], U8, name="w2_scales", align_bytes=ALIGN)
+        h_grouped = []
+        h_banks = []
+        for g in range(groups):
+            bank = psum.tile([P, PACK, GROUP], F32, name=f"h_bank{g}")
+            h_banks.append(bank)
+            tile = keep.tile([P, GROUP, PACK], BF16, name=f"h_grouped{g}", align_bytes=ALIGN)
+            h_grouped.append(tile)
+        y_head = psum.tile([P, 4 * GROUP], F32, name="y_head")
+        y_tail = psum.tile([P, 2 * GROUP], F32, name="y_tail")
+        result = keep.tile([P, S], F32, name="result")
+
+        def last_gather(s):
+            nc.vector.tensor_copy(x_grouped[s][:, :, PACK - 1], planes[PACK - 1][:].indirect(entries(s)))
+
+        def quantize_x(s):
+            cols = slice(s * SLICE, (s + 1) * SLICE)
+            quantize(nc, x_codes[:, cols], x_scales[:, cols], x_grouped[s][:].rearrange("p n t -> p (n t)"))
+
+        def first_layer(g):
+            cols = slice(g * GROUP, (g + 1) * GROUP)
+            for t in range(PACK):
+                w_cols = slice(t * P, (t + 1) * P)
+                nc.tensor.matmul_mx(
+                    out=h_banks[g][:, t, :],
+                    lhsT=w1_codes[:, w_cols].bitcast(FP8X4),
+                    lhsT_scale=w1_scales[:, w_cols],
+                    rhs=x_codes[:, cols].bitcast(FP8X4),
+                    rhs_scale=x_scales[:, cols],
+                    start=True,
+                    stop=True,
+                )
+            nc.scalar.activation(h_grouped[g][:], h_banks[g][:].rearrange("p t n -> p n t"), GELU)
+
+        def quantize_h(g):
+            cols = slice(g * GROUP, (g + 1) * GROUP)
+            quantize(nc, h_codes[:, cols], h_scales[:, cols], h_grouped[g][:].rearrange("p n t -> p (n t)"))
+
+        def second_layer(g):
+            cols = slice(g * GROUP, (g + 1) * GROUP)
+            y = y_head[:, cols] if g < 4 else y_tail[:, (g - 4) * GROUP : (g - 3) * GROUP]
+            nc.tensor.matmul_mx(
+                out=y,
+                lhsT=w2_codes[:].bitcast(FP8X4),
+                lhsT_scale=w2_scales[:],
+                rhs=h_codes[:, cols].bitcast(FP8X4),
+                rhs_scale=h_scales[:, cols],
+                start=True,
+                stop=True,
+            )
+
+        last_gather(0)
+        quantize_x(0)
+        first_layer(0)
+        first_layer(1)
+        last_gather(1)
+        quantize_x(1)
+        first_layer(2)
+        first_layer(3)
+        quantize(nc, w2_codes[:], w2_scales[:], w2_grouped[:].rearrange("p n t -> p (n t)"))
+        last_gather(2)
+        quantize_h(0)
+        quantize_x(2)
+        first_layer(4)
+        first_layer(5)
+        second_layer(0)
+        quantize_h(1)
+        second_layer(1)
+        quantize_h(2)
+        second_layer(2)
+        quantize_h(3)
+        second_layer(3)
+        nc.vector.tensor_copy(result[:, : 4 * GROUP], y_head[:])
+        nc.sync.dma_start(out=out[:, : 4 * GROUP], in_=result[:, : 4 * GROUP])
+        quantize_h(4)
+        second_layer(4)
+        quantize_h(5)
+        second_layer(5)
+        nc.vector.tensor_copy(result[:, 4 * GROUP :], y_tail[:])
+        nc.sync.dma_start(out=out[:, 4 * GROUP :], in_=result[:, 4 * GROUP :])

@@ -18,6 +18,7 @@ PACK = 4
 SLICE = 256
 GROUP = 128
 ALIGN = 64
+W1_SCALAR = 48
 
 
 def quantize(nc, codes, scales, values):
@@ -54,18 +55,14 @@ def tile_picked_pick_mlp_gelu_sub_e_kernel(tc, xT, w1, w2, offs, out):
         nc.scalar.activation(probe_out[:], probe[:], GELU)
 
         early = PACK // 2
-        picked = []
-        for s in range(slices):
-            tile = keep.tile([P, PACK, SLICE], F32, name=f"picked{s}")
-            nc.gpsimd.memset(tile[:, early:, :], 0.0)
-            picked.append(tile)
+        picked = keep.tile([P, PACK, S], F32, name="picked")
+        nc.gpsimd.memset(picked[:, early:, :], 0.0)
 
         w1_grouped = keep.tile([P, H * PACK], BF16, name="w1_grouped", align_bytes=ALIGN)
         w1_to = w1_grouped[:].rearrange("p (t m j) -> p m j t", t=PACK, j=PACK)
         w1_from = w1_raw[:].rearrange("p j (m t) -> p m j t", t=PACK)
-        for half in range(2):
-            part = slice(half * (P // 2), (half + 1) * (P // 2))
-            nc.scalar.copy(w1_to[:, part], w1_from[:, part])
+        nc.scalar.copy(w1_to[:, :W1_SCALAR], w1_from[:, :W1_SCALAR])
+        nc.vector.tensor_copy(w1_to[:, W1_SCALAR:], w1_from[:, W1_SCALAR:])
         w1_codes = keep.tile([P, H], U32, name="w1_codes", align_bytes=ALIGN)
         w1_scales = keep.tile([P, H], U8, name="w1_scales", align_bytes=ALIGN)
         quantize(nc, w1_codes[:], w1_scales[:], w1_grouped[:])
@@ -78,21 +75,32 @@ def tile_picked_pick_mlp_gelu_sub_e_kernel(tc, xT, w1, w2, offs, out):
         def entries(s):
             return offsets[:, s * (SLICE // 16) : (s + 1) * (SLICE // 16)]
 
-        for j in range(early):
-            for s in range(slices):
-                nc.vector.tensor_copy(picked[s][:, j, :], planes[j][:].indirect(entries(s)))
-        for s in range(slices):
+        def part(s):
+            return slice(s * SLICE, (s + 1) * SLICE)
+
+        def gather_plain(j, s):
+            nc.vector.tensor_copy(picked[:, j, part(s)], planes[j][:].indirect(entries(s)))
+
+        def gather_stepped(j, s):
+            nc.vector.tensor_copy(x_grouped[s][:, :, j], planes[j][:].indirect(entries(s)))
+
+        def interleave(s):
             nc.scalar.copy(
                 x_grouped[s][:].rearrange("p (c i) t -> p c t i", i=4),
-                picked[s][:].rearrange("p t (c i) -> p c t i", i=4),
+                picked[:, :, part(s)].rearrange("p t (c i) -> p c t i", i=4),
             )
+
+        nc.vector.tensor_copy(picked[:, 0, :], planes[0][:].indirect(offsets[:]))
         for s in range(slices):
-            nc.vector.tensor_copy(x_grouped[s][:, :, early], planes[early][:].indirect(entries(s)))
+            gather_plain(1, s)
+        interleave(0)
+        gather_plain(2, 1)
+        interleave(1)
+        gather_plain(2, 2)
+        gather_stepped(2, 0)
+        interleave(2)
 
         w2_grouped = keep.tile([P, N, PACK], BF16, name="w2_grouped", align_bytes=ALIGN)
-        nc.scalar.copy(
-            w2_grouped[:].rearrange("p (c i) t -> p c t i", i=4), w2_raw[:].rearrange("p t (c i) -> p c t i", i=4)
-        )
 
         x_codes = keep.tile([P, S], U32, name="x_codes", align_bytes=ALIGN)
         x_scales = keep.tile([P, S], U8, name="x_scales", align_bytes=ALIGN)
@@ -100,23 +108,20 @@ def tile_picked_pick_mlp_gelu_sub_e_kernel(tc, xT, w1, w2, offs, out):
         h_scales = keep.tile([P, S], U8, name="h_scales", align_bytes=ALIGN)
         w2_codes = keep.tile([P, N], U32, name="w2_codes", align_bytes=ALIGN)
         w2_scales = keep.tile([P, N], U8, name="w2_scales", align_bytes=ALIGN)
-        h_grouped = []
+        result = keep.tile([P, S], F32, name="result")
+        y_head = psum.tile([P, 4 * GROUP], F32, name="y_head")
+        y_tail = psum.tile([P, GROUP], F32, name="y_tail")
         h_banks = []
         for g in range(groups):
             bank = psum.tile([P, PACK, GROUP], F32, name=f"h_bank{g}")
             h_banks.append(bank)
-            tile = keep.tile([P, GROUP, PACK], BF16, name=f"h_grouped{g}", align_bytes=ALIGN)
-            h_grouped.append(tile)
-        y_head = psum.tile([P, 4 * GROUP], F32, name="y_head")
-        y_tail = psum.tile([P, 2 * GROUP], F32, name="y_tail")
-        result = keep.tile([P, S], F32, name="result")
+        h_grouped = keep.tile([P, S, PACK], BF16, name="h_grouped", align_bytes=ALIGN)
 
-        def last_gather(s):
-            nc.vector.tensor_copy(x_grouped[s][:, :, PACK - 1], planes[PACK - 1][:].indirect(entries(s)))
-
-        def quantize_x(s):
-            cols = slice(s * SLICE, (s + 1) * SLICE)
-            quantize(nc, x_codes[:, cols], x_scales[:, cols], x_grouped[s][:].rearrange("p n t -> p (n t)"))
+        def quantize_x(start, width):
+            cols = slice(start, start + width)
+            s = start // SLICE
+            own = slice(start % SLICE, start % SLICE + width)
+            quantize(nc, x_codes[:, cols], x_scales[:, cols], x_grouped[s][:, own, :].rearrange("p n t -> p (n t)"))
 
         def first_layer(g):
             cols = slice(g * GROUP, (g + 1) * GROUP)
@@ -131,15 +136,19 @@ def tile_picked_pick_mlp_gelu_sub_e_kernel(tc, xT, w1, w2, offs, out):
                     start=True,
                     stop=True,
                 )
-            nc.scalar.activation(h_grouped[g][:], h_banks[g][:].rearrange("p t n -> p n t"), GELU)
 
-        def quantize_h(g):
-            cols = slice(g * GROUP, (g + 1) * GROUP)
-            quantize(nc, h_codes[:, cols], h_scales[:, cols], h_grouped[g][:].rearrange("p n t -> p (n t)"))
+        def gelu(start, width):
+            cols = slice(start, start + width)
+            own = slice(start % GROUP, start % GROUP + width)
+            bank = h_banks[start // GROUP]
+            nc.scalar.activation(h_grouped[:, cols, :], bank[:, :, own].rearrange("p t n -> p n t"), GELU)
 
-        def second_layer(g):
-            cols = slice(g * GROUP, (g + 1) * GROUP)
-            y = y_head[:, cols] if g < 4 else y_tail[:, (g - 4) * GROUP : (g - 3) * GROUP]
+        def quantize_h(start, width):
+            cols = slice(start, start + width)
+            quantize(nc, h_codes[:, cols], h_scales[:, cols], h_grouped[:, cols, :].rearrange("p n t -> p (n t)"))
+
+        def second_layer(y, start, width):
+            cols = slice(start, start + width)
             nc.tensor.matmul_mx(
                 out=y,
                 lhsT=w2_codes[:].bitcast(FP8X4),
@@ -150,32 +159,48 @@ def tile_picked_pick_mlp_gelu_sub_e_kernel(tc, xT, w1, w2, offs, out):
                 stop=True,
             )
 
-        last_gather(0)
-        quantize_x(0)
+        def hold(s):
+            nc.gpsimd.tensor_copy(x_grouped[s][:, 0, PACK - 1 :], x_grouped[s + 1][:, 0, PACK - 1 :])
+
+        gather_stepped(3, 0)
+        quantize_x(0, GROUP)
+        hold(0)
+        quantize_x(GROUP, GROUP)
         first_layer(0)
+        nc.scalar.copy(
+            w2_grouped[:].rearrange("p (c i) t -> p c t i", i=4), w2_raw[:].rearrange("p t (c i) -> p c t i", i=4)
+        )
+        gelu(0, GROUP)
         first_layer(1)
-        last_gather(1)
-        quantize_x(1)
+        gelu(GROUP, GROUP)
+        gather_stepped(3, 1)
+        quantize_x(SLICE, GROUP)
+        hold(1)
+        quantize_x(SLICE + GROUP, GROUP)
         first_layer(2)
+        gelu(2 * GROUP, GROUP)
         first_layer(3)
+        gelu(3 * GROUP, GROUP)
+        gather_stepped(3, 2)
+        quantize_x(2 * SLICE, SLICE)
         quantize(nc, w2_codes[:], w2_scales[:], w2_grouped[:].rearrange("p n t -> p (n t)"))
-        last_gather(2)
-        quantize_h(0)
-        quantize_x(2)
         first_layer(4)
+        gelu(4 * GROUP, GROUP)
         first_layer(5)
-        second_layer(0)
-        quantize_h(1)
-        second_layer(1)
-        quantize_h(2)
-        second_layer(2)
-        quantize_h(3)
-        second_layer(3)
-        nc.vector.tensor_copy(result[:, : 4 * GROUP], y_head[:])
+        gelu(5 * GROUP, GROUP // 2)
+        gelu(5 * GROUP + GROUP // 2, GROUP // 2)
+        quantize_h(0, SLICE)
+        second_layer(y_head[:, :SLICE], 0, SLICE)
+        quantize_h(SLICE, SLICE)
+        second_layer(y_head[:, SLICE:], SLICE, SLICE)
+        nc.scalar.copy(result[:, : 4 * GROUP], y_head[:])
         nc.sync.dma_start(out=out[:, : 4 * GROUP], in_=result[:, : 4 * GROUP])
-        quantize_h(4)
-        second_layer(4)
-        quantize_h(5)
-        second_layer(5)
-        nc.vector.tensor_copy(result[:, 4 * GROUP :], y_tail[:])
+        quantize_h(4 * GROUP, GROUP)
+        second_layer(y_tail[:], 4 * GROUP, GROUP)
+        nc.scalar.copy(result[:, 4 * GROUP : 5 * GROUP], y_tail[:])
+        y_last = psum.tile([P, GROUP], F32, name="y_last", tag="h_bank0")
+        for start in (0, GROUP // 2):
+            quantize_h(5 * GROUP + start, GROUP // 2)
+            second_layer(y_last[:, start : start + GROUP // 2], 5 * GROUP + start, GROUP // 2)
+        nc.vector.tensor_copy(result[:, 5 * GROUP :], y_last[:])
         nc.sync.dma_start(out=out[:, 4 * GROUP :], in_=result[:, 4 * GROUP :])

@@ -109,8 +109,6 @@ def tile_picked_pick_mlp_gelu_sub_e_kernel(tc, xT, w1, w2, offs, out):
         w2_codes = keep.tile([P, N], U32, name="w2_codes", align_bytes=ALIGN)
         w2_scales = keep.tile([P, N], U8, name="w2_scales", align_bytes=ALIGN)
         result = keep.tile([P, S], F32, name="result")
-        y_head = psum.tile([P, 4 * GROUP], F32, name="y_head")
-        y_tail = psum.tile([P, GROUP], F32, name="y_tail")
         h_banks = []
         for g in range(groups):
             bank = psum.tile([P, PACK, GROUP], F32, name=f"h_bank{g}")
@@ -160,7 +158,7 @@ def tile_picked_pick_mlp_gelu_sub_e_kernel(tc, xT, w1, w2, offs, out):
             )
 
         def hold(s):
-            nc.gpsimd.tensor_copy(x_grouped[s][:, 0, PACK - 1 :], x_grouped[s + 1][:, 0, PACK - 1 :])
+            nc.vector.tensor_copy(x_grouped[s][:, 0, PACK - 1 :], x_grouped[s + 1][:, 0, PACK - 1 :])
 
         gather_stepped(3, 0)
         quantize_x(0, GROUP)
@@ -189,18 +187,22 @@ def tile_picked_pick_mlp_gelu_sub_e_kernel(tc, xT, w1, w2, offs, out):
         first_layer(5)
         gelu(5 * GROUP, GROUP // 2)
         gelu(5 * GROUP + GROUP // 2, GROUP // 2)
-        quantize_h(0, SLICE)
-        second_layer(y_head[:, :SLICE], 0, SLICE)
-        quantize_h(SLICE, SLICE)
-        second_layer(y_head[:, SLICE:], SLICE, SLICE)
-        nc.scalar.copy(result[:, : 4 * GROUP], y_head[:])
-        nc.sync.dma_start(out=out[:, : 4 * GROUP], in_=result[:, : 4 * GROUP])
+        y_banks = []
+        for s in range(2):
+            bank = psum.tile([P, SLICE], F32, name=f"y_bank{s}")
+            y_banks.append(bank)
+        y_fifth = psum.tile([P, GROUP], F32, name="y_fifth", tag="h_bank0")
+        y_sixth = psum.tile([P, GROUP], F32, name="y_sixth", tag="h_bank1")
+        for s in range(2):
+            quantize_h(s * SLICE, SLICE)
+            second_layer(y_banks[s][:], s * SLICE, SLICE)
+            nc.vector.tensor_copy(result[:, part(s)], y_banks[s][:])
+        nc.sync.dma_start(out=out[:, : 2 * SLICE], in_=result[:, : 2 * SLICE])
         quantize_h(4 * GROUP, GROUP)
-        second_layer(y_tail[:], 4 * GROUP, GROUP)
-        nc.scalar.copy(result[:, 4 * GROUP : 5 * GROUP], y_tail[:])
-        y_last = psum.tile([P, GROUP], F32, name="y_last", tag="h_bank0")
+        second_layer(y_fifth[:], 4 * GROUP, GROUP)
+        nc.scalar.copy(result[:, 4 * GROUP : 5 * GROUP], y_fifth[:])
         for start in (0, GROUP // 2):
             quantize_h(5 * GROUP + start, GROUP // 2)
-            second_layer(y_last[:, start : start + GROUP // 2], 5 * GROUP + start, GROUP // 2)
-        nc.vector.tensor_copy(result[:, 5 * GROUP :], y_last[:])
+            second_layer(y_sixth[:, start : start + GROUP // 2], 5 * GROUP + start, GROUP // 2)
+        nc.vector.tensor_copy(result[:, 5 * GROUP :], y_sixth[:])
         nc.sync.dma_start(out=out[:, 4 * GROUP :], in_=result[:, 4 * GROUP :])

@@ -1,6 +1,7 @@
 from contextlib import ExitStack
 
 import concourse.mybir as mybir
+from concourse.masks import make_identity
 
 K, T, S, H, N = 512, 2048, 768, 512, 128
 FLOPS = 2 * S * H * (K + N)
@@ -55,6 +56,9 @@ def tile_picked_pick_mlp_gelu_sub_e_kernel(tc, xT, w1, w2, offs, out):
         nc.scalar.activation(probe_out[:], probe[:], GELU)
 
         early = PACK // 2
+        identity = keep.tile([P, P], F32, name="identity")
+        make_identity(nc, identity[:])
+        warm = psum.tile([P, PACK, P], F32, name="warm", tag="y_bank0")
         picked = keep.tile([P, PACK, S], F32, name="picked")
         nc.gpsimd.memset(picked[:, early:, :], 0.0)
 
@@ -94,6 +98,9 @@ def tile_picked_pick_mlp_gelu_sub_e_kernel(tc, xT, w1, w2, offs, out):
         for s in range(slices):
             gather_plain(1, s)
         interleave(0)
+        for i in range(18):
+            block = slice((i % 16) * P, (i % 16 + 1) * P)
+            nc.tensor.transpose(warm[:, i % PACK, :], planes[2][:, block], identity[:])
         gather_plain(2, 1)
         interleave(1)
         gather_plain(2, 2)
@@ -201,8 +208,9 @@ def tile_picked_pick_mlp_gelu_sub_e_kernel(tc, xT, w1, w2, offs, out):
         quantize_h(4 * GROUP, GROUP)
         second_layer(y_fifth[:], 4 * GROUP, GROUP)
         nc.scalar.copy(result[:, 4 * GROUP : 5 * GROUP], y_fifth[:])
+        nc.sync.dma_start(out=out[:, 4 * GROUP : 5 * GROUP], in_=result[:, 4 * GROUP : 5 * GROUP])
         for start in (0, GROUP // 2):
             quantize_h(5 * GROUP + start, GROUP // 2)
             second_layer(y_sixth[:, start : start + GROUP // 2], 5 * GROUP + start, GROUP // 2)
         nc.vector.tensor_copy(result[:, 5 * GROUP :], y_sixth[:])
-        nc.sync.dma_start(out=out[:, 4 * GROUP :], in_=result[:, 4 * GROUP :])
+        nc.sync.dma_start(out=out[:, 5 * GROUP :], in_=result[:, 5 * GROUP :])

from contextlib import ExitStack

import concourse.mybir as mybir
from concourse.masks import make_identity

K, T, S, H, N = 512, 2048, 768, 512, 128
FLOPS = 2 * S * H * (K + N)

F32 = mybir.dt.float32
BF16 = mybir.dt.bfloat16
U32 = mybir.dt.uint32
U16 = mybir.dt.uint16
U8 = mybir.dt.uint8
FP8X4 = mybir.dt.float8_e4m3fn_x4
GELU = mybir.ActivationFunctionType.Gelu_apprx_tanh

P = 128
PACK = 4
SLICE = 256
GROUP = 128
ALIGN = 64
W1_SCALAR = 48


def quantize(nc, codes, scales, values):
    nc.vector.quantize_mx(out=codes.bitcast(FP8X4), scales=scales, in_=values)


def tile_picked_pick_mlp_gelu_sub_e_kernel(tc, xT, w1, w2, offs, out):
    nc = tc.nc
    slices = S // SLICE
    per_slice = SLICE // GROUP
    groups = S // GROUP

    with ExitStack() as ctx:
        keep = ctx.enter_context(tc.tile_pool(name="keep", bufs=1))
        psum = ctx.enter_context(tc.psum_pool(name="psum", bufs=1))

        offsets = keep.tile([P, S // 16], U16, name="offsets")
        nc.sync.dma_start(offsets[:], offs)

        w1_raw = keep.tile([P, PACK, H], F32, name="w1_raw")
        nc.sync.dma_start(out=w1_raw[:], in_=w1.rearrange("(p j) h -> p j h", j=PACK))
        planes = []
        x_rows = xT.rearrange("(p j) t -> p j t", j=PACK)
        for j in range(PACK):
            plane = keep.tile([P, T], F32, name=f"plane{j}")
            nc.sync.dma_start(out=plane[:], in_=x_rows[:, j, :])
            planes.append(plane)
        w2_raw = keep.tile([P, PACK, N], F32, name="w2_raw")
        nc.sync.dma_start(out=w2_raw[:], in_=w2.rearrange("(p j) n -> p j n", j=PACK))

        probe = keep.tile([P, 1], F32, name="probe")
        nc.vector.memset(probe[:], 0.0)
        probe_out = keep.tile([P, 1], F32, name="probe_out")
        nc.scalar.activation(probe_out[:], probe[:], GELU)

        early = PACK // 2
        identity = keep.tile([P, P], F32, name="identity")
        make_identity(nc, identity[:])
        warm = psum.tile([P, PACK, P], F32, name="warm", tag="y_bank0")
        picked = keep.tile([P, PACK, S], F32, name="picked")
        nc.gpsimd.memset(picked[:, early:, :], 0.0)

        w1_grouped = keep.tile([P, H * PACK], BF16, name="w1_grouped", align_bytes=ALIGN)
        w1_to = w1_grouped[:].rearrange("p (t m j) -> p m j t", t=PACK, j=PACK)
        w1_from = w1_raw[:].rearrange("p j (m t) -> p m j t", t=PACK)
        nc.scalar.copy(w1_to[:, :W1_SCALAR], w1_from[:, :W1_SCALAR])
        nc.vector.tensor_copy(w1_to[:, W1_SCALAR:], w1_from[:, W1_SCALAR:])
        w1_codes = keep.tile([P, H], U32, name="w1_codes", align_bytes=ALIGN)
        w1_scales = keep.tile([P, H], U8, name="w1_scales", align_bytes=ALIGN)
        quantize(nc, w1_codes[:], w1_scales[:], w1_grouped[:])

        x_grouped = []
        for s in range(slices):
            tile = keep.tile([P, SLICE, PACK], BF16, name=f"x_grouped{s}", align_bytes=ALIGN)
            x_grouped.append(tile)

        def entries(s):
            return offsets[:, s * (SLICE // 16) : (s + 1) * (SLICE // 16)]

        def part(s):
            return slice(s * SLICE, (s + 1) * SLICE)

        def gather_plain(j, s):
            nc.vector.tensor_copy(picked[:, j, part(s)], planes[j][:].indirect(entries(s)))

        def gather_stepped(j, s):
            nc.vector.tensor_copy(x_grouped[s][:, :, j], planes[j][:].indirect(entries(s)))

        def interleave(s):
            nc.scalar.copy(
                x_grouped[s][:].rearrange("p (c i) t -> p c t i", i=4),
                picked[:, :, part(s)].rearrange("p t (c i) -> p c t i", i=4),
            )

        nc.vector.tensor_copy(picked[:, 0, :], planes[0][:].indirect(offsets[:]))
        for s in range(slices):
            gather_plain(1, s)
        interleave(0)
        for i in range(18):
            block = slice((i % 16) * P, (i % 16 + 1) * P)
            nc.tensor.transpose(warm[:, i % PACK, :], planes[2][:, block], identity[:])
        gather_plain(2, 1)
        interleave(1)
        gather_plain(2, 2)
        gather_stepped(2, 0)
        interleave(2)

        w2_grouped = keep.tile([P, N, PACK], BF16, name="w2_grouped", align_bytes=ALIGN)

        x_codes = keep.tile([P, S], U32, name="x_codes", align_bytes=ALIGN)
        x_scales = keep.tile([P, S], U8, name="x_scales", align_bytes=ALIGN)
        h_codes = keep.tile([P, S], U32, name="h_codes", align_bytes=ALIGN)
        h_scales = keep.tile([P, S], U8, name="h_scales", align_bytes=ALIGN)
        w2_codes = keep.tile([P, N], U32, name="w2_codes", align_bytes=ALIGN)
        w2_scales = keep.tile([P, N], U8, name="w2_scales", align_bytes=ALIGN)
        result = keep.tile([P, S], F32, name="result")
        h_banks = []
        for g in range(groups):
            bank = psum.tile([P, PACK, GROUP], F32, name=f"h_bank{g}")
            h_banks.append(bank)
        h_grouped = keep.tile([P, S, PACK], BF16, name="h_grouped", align_bytes=ALIGN)

        def quantize_x(start, width):
            cols = slice(start, start + width)
            s = start // SLICE
            own = slice(start % SLICE, start % SLICE + width)
            quantize(nc, x_codes[:, cols], x_scales[:, cols], x_grouped[s][:, own, :].rearrange("p n t -> p (n t)"))

        def first_layer(g):
            cols = slice(g * GROUP, (g + 1) * GROUP)
            for t in range(PACK):
                w_cols = slice(t * P, (t + 1) * P)
                nc.tensor.matmul_mx(
                    out=h_banks[g][:, t, :],
                    lhsT=w1_codes[:, w_cols].bitcast(FP8X4),
                    lhsT_scale=w1_scales[:, w_cols],
                    rhs=x_codes[:, cols].bitcast(FP8X4),
                    rhs_scale=x_scales[:, cols],
                    start=True,
                    stop=True,
                )

        def gelu(start, width):
            cols = slice(start, start + width)
            own = slice(start % GROUP, start % GROUP + width)
            bank = h_banks[start // GROUP]
            nc.scalar.activation(h_grouped[:, cols, :], bank[:, :, own].rearrange("p t n -> p n t"), GELU)

        def quantize_h(start, width):
            cols = slice(start, start + width)
            quantize(nc, h_codes[:, cols], h_scales[:, cols], h_grouped[:, cols, :].rearrange("p n t -> p (n t)"))

        def second_layer(y, start, width):
            cols = slice(start, start + width)
            nc.tensor.matmul_mx(
                out=y,
                lhsT=w2_codes[:].bitcast(FP8X4),
                lhsT_scale=w2_scales[:],
                rhs=h_codes[:, cols].bitcast(FP8X4),
                rhs_scale=h_scales[:, cols],
                start=True,
                stop=True,
            )

        def hold(s):
            nc.vector.tensor_copy(x_grouped[s][:, 0, PACK - 1 :], x_grouped[s + 1][:, 0, PACK - 1 :])

        gather_stepped(3, 0)
        quantize_x(0, GROUP)
        hold(0)
        quantize_x(GROUP, GROUP)
        first_layer(0)
        nc.scalar.copy(
            w2_grouped[:].rearrange("p (c i) t -> p c t i", i=4), w2_raw[:].rearrange("p t (c i) -> p c t i", i=4)
        )
        gelu(0, GROUP)
        first_layer(1)
        gelu(GROUP, GROUP)
        gather_stepped(3, 1)
        quantize_x(SLICE, GROUP)
        hold(1)
        quantize_x(SLICE + GROUP, GROUP)
        first_layer(2)
        gelu(2 * GROUP, GROUP)
        first_layer(3)
        gelu(3 * GROUP, GROUP)
        gather_stepped(3, 2)
        quantize_x(2 * SLICE, SLICE)
        quantize(nc, w2_codes[:], w2_scales[:], w2_grouped[:].rearrange("p n t -> p (n t)"))
        first_layer(4)
        gelu(4 * GROUP, GROUP)
        first_layer(5)
        gelu(5 * GROUP, GROUP // 2)
        gelu(5 * GROUP + GROUP // 2, GROUP // 2)
        y_banks = []
        for s in range(2):
            bank = psum.tile([P, SLICE], F32, name=f"y_bank{s}")
            y_banks.append(bank)
        y_fifth = psum.tile([P, GROUP], F32, name="y_fifth", tag="h_bank0")
        y_sixth = psum.tile([P, GROUP], F32, name="y_sixth", tag="h_bank1")
        for s in range(2):
            quantize_h(s * SLICE, SLICE)
            second_layer(y_banks[s][:], s * SLICE, SLICE)
            nc.vector.tensor_copy(result[:, part(s)], y_banks[s][:])
        nc.sync.dma_start(out=out[:, : 2 * SLICE], in_=result[:, : 2 * SLICE])
        quantize_h(4 * GROUP, GROUP)
        second_layer(y_fifth[:], 4 * GROUP, GROUP)
        nc.scalar.copy(result[:, 4 * GROUP : 5 * GROUP], y_fifth[:])
        nc.sync.dma_start(out=out[:, 4 * GROUP : 5 * GROUP], in_=result[:, 4 * GROUP : 5 * GROUP])
        for start in (0, GROUP // 2):
            quantize_h(5 * GROUP + start, GROUP // 2)
            second_layer(y_sixth[:, start : start + GROUP // 2], 5 * GROUP + start, GROUP // 2)
        nc.vector.tensor_copy(result[:, 5 * GROUP :], y_sixth[:])
        nc.sync.dma_start(out=out[:, 5 * GROUP :], in_=result[:, 5 * GROUP :])
